import numpy as np
import ml_dtypes


def mxq(x, axis, fmt="e4m3"):
    dtype, down = {"e4m3": (ml_dtypes.float8_e4m3fn, 7), "e5m2": (ml_dtypes.float8_e5m2, 14)}[fmt]
    v = np.moveaxis(np.asarray(x, np.float32).astype(ml_dtypes.bfloat16).astype(np.float64), axis, -1)
    blocks = v.reshape(v.shape[:-1] + (-1, 32))
    amax = np.abs(blocks).max(-1, keepdims=True)
    byte = np.maximum(np.where(amax > 0, np.frexp(amax)[1] - 1 + 127, 0) - down, 1)
    scale = np.exp2(byte - 127.0)
    codes = (blocks / scale).astype(np.float32).astype(dtype).astype(np.float64)
    return np.moveaxis((codes * scale).reshape(v.shape), -1, axis)


WIDE = False


def mx_kscale(k):
    if not WIDE:
        return np.ones(k)
    levels = np.array([10, -10, 5, -5, 0])
    if k % 512:
        return np.exp2(np.random.permutation(np.resize(levels, k // 32))).repeat(32)
    a = np.empty((k // 512, 16))
    for p in range(k // 512):
        a[p, :8] = np.random.permutation(np.resize(levels, 8))
        for g in range(8):
            far = levels[np.abs(levels - a[p, g]) >= 10]
            a[p, g + 8] = far[np.random.randint(len(far))]
    return np.exp2(a.ravel()).repeat(32)


def f64(x):
    return np.asarray(x).astype(np.float64)


def striped8(idx):
    return np.concatenate([x.reshape(-1, 16).T for x in idx]).astype(np.uint16)


def runs(offs, k):
    lists = np.stack([offs[16 * r : 16 * r + 16].T.reshape(-1) for r in range(8)]).astype(np.int64)
    return lists[np.arange(k) % 512 // 64]


def pack_weight(w):
    k, n = w.shape
    w = f64(np.asarray(w, np.float32).astype(ml_dtypes.bfloat16)).reshape(k // 32, 32, n)
    amax = np.abs(w).max(1)
    byte = np.clip(np.where(amax > 0, np.frexp(amax)[1] - 1 + 127 - 7, 1), 1, 254)
    scaled = (w * np.exp2(127.0 - byte)[:, None, :]).reshape(k, n).astype(np.float32)
    words = np.ascontiguousarray(scaled.reshape(k // 512, 128, 4, n).transpose(0, 1, 3, 2)).astype(ml_dtypes.float8_e4m3fn).view(np.uint8)
    return words, np.ascontiguousarray(byte.astype(np.uint8).reshape(k // 512, 16, n))


def unpack_weight(words, scales):
    g, p, n, _ = words.shape
    vals = np.ascontiguousarray(words).view(ml_dtypes.float8_e4m3fn).astype(np.float64) * np.repeat(np.exp2(scales.astype(np.float64) - 127.0), 8, axis=1)[..., None]
    return vals.transpose(0, 1, 3, 2).reshape(g * 512, n)


E2M1 = np.array([0.0, 0.5, 1.0, 1.5, 2.0, 3.0, 4.0, 6.0, -0.0, -0.5, -1.0, -1.5, -2.0, -3.0, -4.0, -6.0])


def pack_fp4(w):
    k, n = w.shape
    w = f64(np.asarray(w, np.float32).astype(ml_dtypes.bfloat16)).reshape(k // 32, 32, n)
    amax = np.abs(w).max(1)
    mant, ex = np.frexp(amax / 6.0)
    byte = np.clip(np.where(amax > 0, np.where(mant > 0.5, ex, ex - 1) + 127, 1), 1, 254)
    scaled = (w * np.exp2(127.0 - byte)[:, None, :]).reshape(k, n).astype(np.float32)
    c = np.ascontiguousarray(scaled.reshape(k // 512, 128, 4, n).transpose(0, 1, 3, 2)).astype(ml_dtypes.float4_e2m1fn).view(np.uint8) & 0xF
    words = (c[..., 0::2] | (c[..., 1::2] << 4)).reshape(k // 512, 128, 2 * n)
    return np.ascontiguousarray(words), np.ascontiguousarray(byte.astype(np.uint8).reshape(k // 512, 16, n))


def unpack_fp4(words, scales):
    g, _, n = scales.shape
    words = np.ascontiguousarray(words).reshape(g, 128, n, 2)
    nib = np.empty((g, 128, n, 4), np.uint8)
    nib[..., 0::2] = words & 0xF
    nib[..., 1::2] = words >> 4
    vals = E2M1[nib] * np.repeat(np.exp2(scales.astype(np.float64) - 127.0), 8, axis=1)[..., None]
    return vals.transpose(0, 1, 3, 2).reshape(g * 512, n)


def planes(y):
    n, m = y.shape
    v = y.astype(np.float32).astype(ml_dtypes.bfloat16).astype(np.float64).reshape(n // 32, 32, m)
    top = np.abs(v).max(1)
    byte = np.clip(np.where(top > 0, np.frexp(top)[1] - 1 + 127 - 7, 1), 1, 254)
    codes = (v * np.exp2(127.0 - byte)[:, None, :]).reshape(n, m).astype(np.float32).astype(ml_dtypes.float8_e4m3fn).view(np.uint8)
    words = codes.reshape(n // 512, 128, 4, m).transpose(0, 1, 3, 2)
    return np.ascontiguousarray(words), np.ascontiguousarray(byte.astype(np.uint8).reshape(n // 512, 16, m))


K, T, S, H, C = 512, 2048, 512, 512, 512


def setup_inputs():
    n = np.random.standard_normal
    s = mx_kscale(K)[:, None]
    packed_xT = pack_weight(n((K, T)) * s)
    packed_w1 = pack_fp4(n((K, H)) / np.sqrt(K) / s)
    return {
        "x_words": packed_xT[0],
        "x_scales": packed_xT[1],
        "w1_words": packed_w1[0],
        "w1_scales": packed_w1[1],
        "gs": (np.random.uniform(0.5, 1.5, (K, 1)) / s).astype(np.float32),
        "offs": striped8(np.random.randint(0, T, (8, S))),
        "n1": striped8(np.stack([np.random.permutation(S) for _ in range(8)])),
        "n2": striped8(np.stack([np.random.permutation(S) for _ in range(8)])),
        "n3": striped8(np.stack([np.random.permutation(S) for _ in range(8)])),
        "n4": striped8(np.stack([np.random.permutation(S) for _ in range(8)])),
        "cand": striped8(np.random.randint(0, T, (8, C))),
        "n5": striped8(np.stack([np.random.permutation(S) for _ in range(8)])),
        "n6": striped8(np.stack([np.random.permutation(S) for _ in range(8)])),
        "n7": striped8(np.stack([np.random.permutation(S) for _ in range(8)])),
    }


def reference(x_words, x_scales, w1_words, w1_scales, gs, offs, n1, n2, n3, n4, cand, n5, n6, n7):
    x_cand = unpack_weight(x_words, x_scales)[np.arange(K)[:, None], runs(cand, K)]
    xq = unpack_weight(x_words, x_scales)[np.arange(K)[:, None], runs(offs, K)]
    y = unpack_fp4(w1_words, w1_scales).T @ xq
    z = f64(gs) * (0.75 * ((y[np.arange(H)[:, None], runs(n1, H)]) * (y[np.arange(H)[:, None], runs(n2, H)]) - ((y[np.arange(H)[:, None], runs(n3, H)]) * (y[np.arange(H)[:, None], runs(n4, H)]))))
    s = 0.0625 * ((x_cand.T @ mxq(z, 0, "e4m3")))
    out_0 = 0.75 * (s * (s[np.arange(C)[:, None], runs(n5, C)]) + (s[np.arange(C)[:, None], runs(n6, C)]) * (s[np.arange(C)[:, None], runs(n7, C)]))
    return (out_0,) + planes(out_0)

@@ -1,0 +1,209 @@
+from contextlib import ExitStack
+
+import concourse.mybir as mybir
+
+F32 = mybir.dt.float32
+BF16 = mybir.dt.bfloat16
+I32 = mybir.dt.int32
+U32 = mybir.dt.uint32
+U16 = mybir.dt.uint16
+U8 = mybir.dt.uint8
+FP8X4 = mybir.dt.float8_e4m3fn_x4
+FP4X4 = mybir.dt.float4_e2m1fn_x4
+MULT = mybir.AluOpType.mult
+ADD = mybir.AluOpType.add
+SUB = mybir.AluOpType.subtract
+COPY = mybir.ActivationFunctionType.Copy
+
+P = 128
+PACK = 4
+T = 2048
+S = 512
+FLOPS = 2 * 2 * 512 * 512 * 512
+
+PIECES = ((0, 384), (384, 512))
+SPANS = {384: ((0, 256), (256, 384)), 128: ((0, 128),)}
+
+
+def tile_picked_hcanddetdot_none_po_kernel(
+    tc, x_words, x_scales, w1_words, w1_scales, gs, offs, n1, n2, n3, n4, cand, n5, n6, n7, out_0, out_1, out_2
+):
+    nc = tc.nc
+    with ExitStack() as ctx:
+        keep = ctx.enter_context(tc.tile_pool(name="keep", bufs=1))
+        psum = ctx.enter_context(tc.psum_pool(name="psum", bufs=1))
+
+        def tile(shape, dtype, name, tag=None):
+            return keep.tile(shape, dtype, name=name, tag=tag or name, align_bytes=64)
+
+        lists = {}
+
+        def load_list(name, source):
+            lists[name] = tile([P, S // 16], U16, "list_" + name)
+            nc.sync.dma_start(lists[name][:], source)
+
+        def entries(name, lo, hi):
+            return lists[name][:, lo // 16 : hi // 16]
+
+        table_scales = tile([P, T], U8, "table_scales")
+        table_words = tile([P, T], U32, "table_words")
+        w_words_in = tile([P, 2 * S], U8, "w_words_in")
+        w_scales_in = tile([P, S], U8, "w_scales_in")
+        place_scales = tile([P, S], U8, "place_scales")
+        cand_scales = tile([P, S], U8, "cand_scales")
+        gain_in = tile([P, PACK], F32, "gain_in")
+        gain = tile([P, PACK], F32, "gain")
+
+        for plane in (table_scales, w_scales_in, place_scales, cand_scales):
+            nc.gpsimd.memset(plane[:].bitcast(I32), 0)
+
+        nc.sync.dma_start(w_words_in[:].bitcast(I32), w1_words[0].bitcast(I32))
+        load_list("offs", offs)
+        scale_rows = x_scales[0].bitcast(I32)
+        for e in range(2):
+            nc.scalar.dma_start(table_scales[:].bitcast(I32)[e:P:16, :], scale_rows[e:16:2, :])
+        nc.sync.dma_start(table_words[:].bitcast(I32), x_words[0].rearrange("p n t -> p (n t)").bitcast(I32))
+        load_list("cand", cand)
+        w_rows = w1_scales[0].bitcast(I32)
+        for a in range(4):
+            nc.scalar.dma_start(w_scales_in[:].bitcast(I32)[a:P:32, :], w_rows[a:16:4, :])
+        nc.sync.dma_start(gain_in[:], gs.rearrange("(p t) o -> p (t o)", t=PACK))
+        nc.scalar.activation(gain[:], gain_in[:], COPY, scale=0.75)
+
+        w_words = tile([P, 2 * S], U8, "w_words")
+        w_scales = tile([P, S], U8, "w_scales")
+        nc.vector.tensor_copy(
+            w_words[:].rearrange("p (t m b) -> p t m b", t=PACK, b=2),
+            w_words_in[:].rearrange("p (m t b) -> p t m b", t=PACK, b=2),
+        )
+
+        def place_rows(plane, gathered, queues):
+            for a in range(4):
+                start = a if a < 2 else 14 + a
+                queues[a % len(queues)].dma_start(plane[:].bitcast(I32)[a:P:32, :], gathered[:].bitcast(I32)[start:P:32, :])
+
+        place_bytes = tile([P, S], U8, "place_bytes")
+        nc.vector.tensor_copy(place_bytes[:], table_scales[:].indirect(lists["offs"][:]))
+        place_rows(place_scales, place_bytes, (nc.sync, nc.scalar))
+
+        for name, source in (("n1", n1), ("n3", n3), ("n2", n2), ("n4", n4)):
+            load_list(name, source)
+
+        place_words = tile([P, S], U32, "place_words")
+        nc.vector.tensor_copy(place_words[:], table_words[:].indirect(lists["offs"][:]))
+        nc.vector.tensor_copy(
+            w_scales[:].rearrange("p (t m) -> p t m", t=PACK), w_scales_in[:].rearrange("p (m t) -> p t m", t=PACK)
+        )
+
+        y = [tile([P, S], F32, "y%d" % t) for t in range(PACK)]
+        yg = [tile([P, S], F32, "yg%d" % t) for t in range(PACK)]
+        for t in range(PACK):
+            bank = psum.tile([P, S], F32, name="y_bank%d" % t)
+            nc.tensor.matmul_mx(
+                out=bank[:],
+                lhsT=w_words[:, 2 * P * t : 2 * P * (t + 1)].bitcast(FP4X4),
+                lhsT_scale=w_scales[:, P * t : P * (t + 1)],
+                rhs=place_words[:].bitcast(FP8X4),
+                rhs_scale=place_scales[:],
+                start=True,
+                stop=True,
+            )
+            nc.scalar.activation(yg[t][:], bank[:], COPY, scale=gain[:, t : t + 1])
+            nc.scalar.copy(y[t][:], bank[:])
+
+        cand_bytes = tile([P, S], U8, "cand_bytes")
+        cand_bytes_dealt = tile([P, S], U8, "cand_bytes_dealt")
+        cand_picked = tile([P, S], U32, "cand_picked")
+        cand_words = tile([P, S], U32, "cand_words")
+        nc.vector.tensor_copy(cand_bytes[:], table_scales[:].indirect(lists["cand"][:]))
+        nc.vector.tensor_copy(cand_picked[:], table_words[:].indirect(lists["cand"][:]))
+        nc.vector.tensor_copy(
+            cand_bytes_dealt[:].rearrange("p (t m) -> p t m", t=PACK), cand_bytes[:].rearrange("p (m t) -> p t m", t=PACK)
+        )
+        nc.vector.tensor_copy(
+            cand_words[:].rearrange("p (t m) -> p t m", t=PACK), cand_picked[:].rearrange("p (m t) -> p t m", t=PACK)
+        )
+        place_rows(cand_scales, cand_bytes_dealt, (nc.sync,))
+        for name, source in (("n6", n6), ("n5", n5), ("n7", n7)):
+            load_list(name, source)
+
+        def interleave(values, width, last, name):
+            grouped = tile([P, width * PACK], BF16, name)
+            target = grouped[:].rearrange("p (c i t) -> p c t i", i=4, t=PACK)
+            source = values[:].rearrange("p (t c i) -> p c t i", i=4, t=PACK)
+            if last:
+                nc.vector.tensor_copy(target, source)
+            else:
+                nc.scalar.copy(target, source)
+            return grouped
+
+        def quantize(words, scales, grouped, lo, width):
+            for a, b in SPANS[width]:
+                nc.vector.quantize_mx(
+                    out=words[:, lo + a : lo + b].bitcast(FP8X4),
+                    scales=scales[:, lo + a : lo + b],
+                    in_=grouped[:, PACK * a : PACK * b],
+                )
+
+        z_words = tile([P, S], U32, "z_words")
+        z_scales = tile([P, S], U8, "z_scales")
+        s = [tile([P, S], F32, "s%d" % t) for t in range(PACK)]
+        sq = [tile([P, S], F32, "sq%d" % t) for t in range(PACK)]
+        s_banks = [psum.tile([P, S], F32, name="s_bank%d" % t) for t in range(PACK)]
+        for lo, hi in PIECES:
+            width = hi - lo
+            z = tile([P, PACK * width], F32, "z%d" % lo)
+            pending = []
+            for t in range(PACK):
+                f3, p12, p34 = [tile([P, width], F32, "%s_%d_%d" % (n, lo, t)) for n in ("f3", "p12", "p34")]
+                f1 = tile([P, width], F32, "f1_%d_%d" % (lo, t), "z_grouped0" if lo > 0 and t == 2 else None)
+                nc.vector.tensor_copy(f1[:], yg[t][:].indirect(entries("n1", lo, hi)))
+                for args in pending:
+                    nc.vector.tensor_tensor(*args)
+                nc.vector.tensor_copy(f3[:], yg[t][:].indirect(entries("n3", lo, hi)))
+                nc.vector.tensor_tensor(p12[:], y[t][:].indirect(entries("n2", lo, hi)), f1[:], MULT)
+                nc.vector.tensor_tensor(p34[:], y[t][:].indirect(entries("n4", lo, hi)), f3[:], MULT)
+                pending = [(z[:, t * width : (t + 1) * width], p12[:], p34[:], SUB)]
+            nc.vector.tensor_tensor(*pending[0])
+            grouped = interleave(z, width, hi == S, "z_grouped%d" % lo)
+            quantize(z_words, z_scales, grouped, lo, width)
+            for t in range(PACK):
+                for a, b in SPANS[width]:
+                    nc.tensor.matmul_mx(
+                        out=s_banks[t][:, lo + a : lo + b],
+                        lhsT=cand_words[:, P * t : P * (t + 1)].bitcast(FP8X4),
+                        lhsT_scale=cand_scales[:, P * t : P * (t + 1)],
+                        rhs=z_words[:, lo + a : lo + b].bitcast(FP8X4),
+                        rhs_scale=z_scales[:, lo + a : lo + b],
+                        start=True,
+                        stop=True,
+                    )
+                nc.scalar.activation(sq[t][:, lo:hi], s_banks[t][:, lo:hi], COPY, scale=0.75 * 0.0625)
+                nc.scalar.activation(s[t][:, lo:hi], s_banks[t][:, lo:hi], COPY, scale=0.0625)
+
+        o_words = tile([P, S], U32, "o_words")
+        o_scales = tile([P, S], U8, "o_scales")
+        out_rows = out_0.rearrange("(p t) j -> p t j", t=PACK)
+        out_words = out_1[0].rearrange("p n t -> p (n t)").bitcast(I32)
+        for lo, hi in PIECES:
+            width = hi - lo
+            o = tile([P, PACK * width], F32, "o%d" % lo)
+            pending = []
+            for t in range(PACK):
+                p5, p67 = [tile([P, width], F32, "%s_%d_%d" % (n, lo, t)) for n in ("p5", "p67")]
+                f6 = tile([P, width], F32, "f6_%d_%d" % (lo, t), "o_grouped0" if lo > 0 and t == 3 else None)
+                nc.vector.tensor_copy(f6[:], sq[t][:].indirect(entries("n6", lo, hi)))
+                for args in pending:
+                    nc.vector.tensor_tensor(*args)
+                nc.vector.tensor_tensor(p5[:], s[t][:].indirect(entries("n5", lo, hi)), sq[t][:, lo:hi], MULT)
+                nc.vector.tensor_tensor(p67[:], s[t][:].indirect(entries("n7", lo, hi)), f6[:], MULT)
+                pending = [(o[:, t * width : (t + 1) * width], p5[:], p67[:], ADD)]
+            nc.vector.tensor_tensor(*pending[0])
+            nc.sync.dma_start(out_rows[:, :, lo:hi], o[:].rearrange("p (t j) -> p t j", t=PACK))
+            grouped = interleave(o, width, hi == S, "o_grouped%d" % lo)
+            quantize(o_words, o_scales, grouped, lo, width)
+            nc.sync.dma_start(out_words[:, lo:hi], o_words[:].bitcast(I32)[:, lo:hi])
+        out_scale_rows = out_2[0].bitcast(I32)
+        for q in range(4):
+            queue = nc.scalar if q % 2 == 0 else nc.sync
+            queue.dma_start(out_scale_rows[4 * q : 4 * q + 4, :], o_scales[:].bitcast(I32)[32 * q : 32 * q + 4, :])

@@ -154,17 +154,18 @@ def tile_picked_hcanddetdot_none_po_kernel(
             width = hi - lo
             z = tile([P, PACK * width], F32, "z%d" % lo)
             pending = []
+            joiner = nc.vector if hi == S else nc.gpsimd
             for t in range(PACK):
-                f3, p12, p34 = [tile([P, width], F32, "%s_%d_%d" % (n, lo, t)) for n in ("f3", "p12", "p34")]
-                f1 = tile([P, width], F32, "f1_%d_%d" % (lo, t), "z_grouped0" if lo > 0 and t == 2 else None)
+                f1, p12, p34 = [tile([P, width], F32, "%s_%d_%d" % (n, lo, t)) for n in ("f1", "p12", "p34")]
+                f3 = tile([P, width], F32, "f3_%d_%d" % (lo, t), "z_grouped0" if lo > 0 and t == 3 else None)
                 nc.vector.tensor_copy(f1[:], yg[t][:].indirect(entries("n1", lo, hi)))
                 for args in pending:
-                    nc.vector.tensor_tensor(*args)
+                    joiner.tensor_tensor(*args)
                 nc.vector.tensor_copy(f3[:], yg[t][:].indirect(entries("n3", lo, hi)))
                 nc.vector.tensor_tensor(p12[:], y[t][:].indirect(entries("n2", lo, hi)), f1[:], MULT)
                 nc.vector.tensor_tensor(p34[:], y[t][:].indirect(entries("n4", lo, hi)), f3[:], MULT)
                 pending = [(z[:, t * width : (t + 1) * width], p12[:], p34[:], SUB)]
-            nc.vector.tensor_tensor(*pending[0])
+            joiner.tensor_tensor(*pending[0])
             grouped = interleave(z, width, hi == S, "z_grouped%d" % lo)
             quantize(z_words, z_scales, grouped, lo, width)
             for t in range(PACK):
@@ -178,8 +179,12 @@ def tile_picked_hcanddetdot_none_po_kernel(
                         start=True,
                         stop=True,
                     )
-                nc.scalar.activation(sq[t][:, lo:hi], s_banks[t][:, lo:hi], COPY, scale=0.75 * 0.0625)
-                nc.scalar.activation(s[t][:, lo:hi], s_banks[t][:, lo:hi], COPY, scale=0.0625)
+                if t == 0:
+                    nc.scalar.activation(sq[t][:, lo:hi], s_banks[t][:, lo:hi], COPY, scale=0.75 * 0.0625)
+                    nc.scalar.activation(s[t][:, lo:hi], s_banks[t][:, lo:hi], COPY, scale=0.0625)
+        for t in range(1, PACK):
+            nc.scalar.activation(sq[t][:], s_banks[t][:], COPY, scale=0.75 * 0.0625)
+            nc.scalar.activation(s[t][:], s_banks[t][:], COPY, scale=0.0625)
 
         o_words = tile([P, S], U32, "o_words")
         o_scales = tile([P, S], U8, "o_scales")
@@ -189,16 +194,17 @@ def tile_picked_hcanddetdot_none_po_kernel(
             width = hi - lo
             o = tile([P, PACK * width], F32, "o%d" % lo)
             pending = []
+            joiner = nc.vector if hi == S else nc.gpsimd
             for t in range(PACK):
-                p5, p67 = [tile([P, width], F32, "%s_%d_%d" % (n, lo, t)) for n in ("p5", "p67")]
-                f6 = tile([P, width], F32, "f6_%d_%d" % (lo, t), "o_grouped0" if lo > 0 and t == 3 else None)
+                f6, p5 = [tile([P, width], F32, "%s_%d_%d" % (n, lo, t)) for n in ("f6", "p5")]
+                p67 = tile([P, width], F32, "p67_%d_%d" % (lo, t), "o_grouped0" if lo > 0 and t == 3 else None)
                 nc.vector.tensor_copy(f6[:], sq[t][:].indirect(entries("n6", lo, hi)))
                 for args in pending:
-                    nc.vector.tensor_tensor(*args)
+                    joiner.tensor_tensor(*args)
                 nc.vector.tensor_tensor(p5[:], s[t][:].indirect(entries("n5", lo, hi)), sq[t][:, lo:hi], MULT)
                 nc.vector.tensor_tensor(p67[:], s[t][:].indirect(entries("n7", lo, hi)), f6[:], MULT)
                 pending = [(o[:, t * width : (t + 1) * width], p5[:], p67[:], ADD)]
-            nc.vector.tensor_tensor(*pending[0])
+            joiner.tensor_tensor(*pending[0])
             nc.sync.dma_start(out_rows[:, :, lo:hi], o[:].rearrange("p (t j) -> p t j", t=PACK))
             grouped = interleave(o, width, hi == S, "o_grouped%d" % lo)
             quantize(o_words, o_scales, grouped, lo, width)

@@ -1,6 +1,7 @@
 from contextlib import ExitStack
 
 import concourse.mybir as mybir
+from concourse.masks import make_identity
 
 F32 = mybir.dt.float32
 BF16 = mybir.dt.bfloat16
@@ -12,7 +13,6 @@ FP8X4 = mybir.dt.float8_e4m3fn_x4
 FP4X4 = mybir.dt.float4_e2m1fn_x4
 MULT = mybir.AluOpType.mult
 ADD = mybir.AluOpType.add
-SUB = mybir.AluOpType.subtract
 COPY = mybir.ActivationFunctionType.Copy
 
 P = 128
@@ -21,8 +21,9 @@ T = 2048
 S = 512
 FLOPS = 2 * 2 * 512 * 512 * 512
 
-PIECES = ((0, 384), (384, 512))
-SPANS = {384: ((0, 256), (256, 384)), 128: ((0, 128),)}
+CHUNKS = 3
+WIDE = CHUNKS * P
+HALF = 256
 
 
 def tile_picked_hcanddetdot_none_po_kernel(
@@ -53,22 +54,26 @@ def tile_picked_hcanddetdot_none_po_kernel(
         cand_scales = tile([P, S], U8, "cand_scales")
         gain_in = tile([P, PACK], F32, "gain_in")
         gain = tile([P, PACK], F32, "gain")
+        minus_gain = tile([P, PACK], F32, "minus_gain")
 
         for plane in (table_scales, w_scales_in, place_scales, cand_scales):
             nc.gpsimd.memset(plane[:].bitcast(I32), 0)
 
         nc.sync.dma_start(w_words_in[:].bitcast(I32), w1_words[0].bitcast(I32))
         load_list("offs", offs)
-        scale_rows = x_scales[0].bitcast(I32)
-        for e in range(2):
-            nc.scalar.dma_start(table_scales[:].bitcast(I32)[e:P:16, :], scale_rows[e:16:2, :])
-        nc.sync.dma_start(table_words[:].bitcast(I32), x_words[0].rearrange("p n t -> p (n t)").bitcast(I32))
+        nc.sync.dma_start(table_scales[:].bitcast(I32)[0:P:8, :], x_scales[0].bitcast(I32))
         load_list("cand", cand)
+        nc.sync.dma_start(gain_in[:], gs.rearrange("(p t) o -> p (t o)", t=PACK))
+        load_list("n1", n1)
+        load_list("n3", n3)
+        nc.sync.dma_start(table_words[:].bitcast(I32), x_words[0].rearrange("p n t -> p (n t)").bitcast(I32))
         w_rows = w1_scales[0].bitcast(I32)
         for a in range(4):
-            nc.scalar.dma_start(w_scales_in[:].bitcast(I32)[a:P:32, :], w_rows[a:16:4, :])
-        nc.sync.dma_start(gain_in[:], gs.rearrange("(p t) o -> p (t o)", t=PACK))
+            nc.sync.dma_start(w_scales_in[:].bitcast(I32)[a:P:32, :], w_rows[a:16:4, :])
         nc.scalar.activation(gain[:], gain_in[:], COPY, scale=0.75)
+        nc.scalar.activation(minus_gain[:], gain_in[:], COPY, scale=-0.75)
+        identity = tile([P, P], F32, "identity")
+        make_identity(nc, identity[:])
 
         w_words = tile([P, 2 * S], U8, "w_words")
         w_scales = tile([P, S], U8, "w_scales")
@@ -79,14 +84,13 @@ def tile_picked_hcanddetdot_none_po_kernel(
 
         def place_rows(plane, gathered, queues):
             for a in range(4):
-                start = a if a < 2 else 14 + a
-                queues[a % len(queues)].dma_start(plane[:].bitcast(I32)[a:P:32, :], gathered[:].bitcast(I32)[start:P:32, :])
+                queues[a % len(queues)].dma_start(plane[:].bitcast(I32)[a:P:32, :], gathered[:].bitcast(I32)[8 * a : P : 32, :])
 
         place_bytes = tile([P, S], U8, "place_bytes")
         nc.vector.tensor_copy(place_bytes[:], table_scales[:].indirect(lists["offs"][:]))
-        place_rows(place_scales, place_bytes, (nc.sync, nc.scalar))
+        place_rows(place_scales, place_bytes, (nc.scalar,))
 
-        for name, source in (("n1", n1), ("n3", n3), ("n2", n2), ("n4", n4)):
+        for name, source in (("n2", n2), ("n4", n4)):
             load_list(name, source)
 
         place_words = tile([P, S], U32, "place_words")
@@ -97,8 +101,9 @@ def tile_picked_hcanddetdot_none_po_kernel(
 
         y = [tile([P, S], F32, "y%d" % t) for t in range(PACK)]
         yg = [tile([P, S], F32, "yg%d" % t) for t in range(PACK)]
+        yn = [tile([P, S], F32, "yn%d" % t) for t in range(PACK)]
         for t in range(PACK):
-            bank = psum.tile([P, S], F32, name="y_bank%d" % t)
+            bank = psum.tile([P, S], F32, name="y_bank%d" % t, tag="bank%d" % t)
             nc.tensor.matmul_mx(
                 out=bank[:],
                 lhsT=w_words[:, 2 * P * t : 2 * P * (t + 1)].bitcast(FP4X4),
@@ -109,11 +114,12 @@ def tile_picked_hcanddetdot_none_po_kernel(
                 stop=True,
             )
             nc.scalar.activation(yg[t][:], bank[:], COPY, scale=gain[:, t : t + 1])
+            nc.scalar.activation(yn[t][:], bank[:], COPY, scale=minus_gain[:, t : t + 1])
             nc.scalar.copy(y[t][:], bank[:])
 
         cand_bytes = tile([P, S], U8, "cand_bytes")
         cand_bytes_dealt = tile([P, S], U8, "cand_bytes_dealt")
-        cand_picked = tile([P, S], U32, "cand_picked")
+        cand_picked = tile([P, S], U32, "cand_picked", "w_scales_in")
         cand_words = tile([P, S], U32, "cand_words")
         nc.vector.tensor_copy(cand_bytes[:], table_scales[:].indirect(lists["cand"][:]))
         nc.vector.tensor_copy(cand_picked[:], table_words[:].indirect(lists["cand"][:]))
@@ -127,89 +133,123 @@ def tile_picked_hcanddetdot_none_po_kernel(
         for name, source in (("n6", n6), ("n5", n5), ("n7", n7)):
             load_list(name, source)
 
-        def interleave(values, width, last, name):
-            grouped = tile([P, width * PACK], BF16, name)
-            target = grouped[:].rearrange("p (c i t) -> p c t i", i=4, t=PACK)
-            source = values[:].rearrange("p (t c i) -> p c t i", i=4, t=PACK)
-            if last:
-                nc.vector.tensor_copy(target, source)
-            else:
-                nc.scalar.copy(target, source)
-            return grouped
+        def quantize(words, scales, grouped, lo, hi):
+            nc.vector.quantize_mx(out=words[:, lo:hi].bitcast(FP8X4), scales=scales[:, lo:hi], in_=grouped[:])
 
-        def quantize(words, scales, grouped, lo, width):
-            for a, b in SPANS[width]:
-                nc.vector.quantize_mx(
-                    out=words[:, lo + a : lo + b].bitcast(FP8X4),
-                    scales=scales[:, lo + a : lo + b],
-                    in_=grouped[:, PACK * a : PACK * b],
-                )
+        def add_on_tensor(left, right, t, sums, name):
+            turned = psum.tile([P, WIDE], F32, name=name + "_turned%d" % t, tag="bank0")
+            for c in range(CHUNKS):
+                cols = slice(c * P, (c + 1) * P)
+                nc.tensor.matmul(turned[:, cols], left[:, cols], identity[:], start=True, stop=False, is_transpose=True)
+                nc.tensor.matmul(turned[:, cols], right[:, cols], identity[:], start=False, stop=True, is_transpose=True)
+            staged = tile([P, WIDE], F32, name + "_staged%d" % t)
+            nc.scalar.copy(staged[:], turned[:])
+            for c in range(CHUNKS):
+                nc.tensor.transpose(sums[c][:, t * P : (t + 1) * P], staged[:, c * P : (c + 1) * P], identity[:])
+
+        def join(products, copies, name, words, scales, store_rows, quantized):
+            sums = [psum.tile([P, PACK * P], F32, name=name + "_sums%d" % c, tag="bank%d" % (c + 1)) for c in range(CHUNKS)]
+            for t in range(PACK):
+                left = tile([P, WIDE], F32, name + "_left%d" % t)
+                right = tile([P, WIDE], F32, name + "_right%d" % t)
+                fetched = [tile([P, WIDE], F32, name + "_fetched%d_%d" % (t, k)) for k in range(copies)]
+                products(t, 0, WIDE, left[:], right[:], [f[:] for f in fetched])
+                add_on_tensor(left, right, t, sums, name)
+                if t < PACK - 1:
+                    store_rows(sums, t)
+            for lo, hi in ((0, HALF), (HALF, WIDE)):
+                grouped = tile([P, (hi - lo) * PACK], BF16, name + "_grouped%d" % lo)
+                for c in range(lo // P, hi // P):
+                    nc.scalar.copy(
+                        grouped[:, (c * P - lo) * PACK : ((c + 1) * P - lo) * PACK].rearrange("p (j t) -> p j t", t=PACK),
+                        sums[c][:].rearrange("p (t j) -> p j t", t=PACK),
+                    )
+                quantize(words, scales, grouped, lo, hi)
+                quantized(lo, hi, None)
+            store_rows(sums, PACK - 1)
+
+            work = tile([P, (2 + copies) * S], F32, name + "_last_work", name + "_fetched%d_0" % (PACK - 1))
+            left, right = work[:, 0:S], work[:, S : 2 * S]
+            final_right = tile([P, P], F32, name + "_final_right", name + "_grouped0")
+            total = tile([P, PACK * P], F32, name + "_last_total")
+            early = slice(0, (PACK - 1) * P)
+            for t in range(PACK):
+                cols = slice(t * P, (t + 1) * P)
+                fetched = [work[:, (2 + k) * S + t * P : (2 + k) * S + (t + 1) * P] for k in range(copies)]
+                products(t, WIDE, S, left[:, cols], right[:, cols] if t < PACK - 1 else final_right[:], fetched)
+                if t == PACK - 2:
+                    nc.vector.tensor_tensor(total[:, early], left[:, early], right[:, early], ADD)
+            nc.vector.tensor_tensor(total[:, cols], left[:, cols], final_right[:], ADD)
+            grouped = tile([P, P * PACK], BF16, name + "_last_grouped", name + "_grouped%d" % HALF)
+            nc.vector.tensor_copy(
+                grouped[:].rearrange("p (c i t) -> p c t i", i=4, t=PACK),
+                total[:].rearrange("p (t c i) -> p c t i", i=4, t=PACK),
+            )
+            quantize(words, scales, grouped, WIDE, S)
+            quantized(WIDE, S, total)
+
+        def z_products(t, lo, hi, left, right, fetched):
+            nc.vector.tensor_copy(fetched[0], yg[t][:].indirect(entries("n1", lo, hi)))
+            nc.vector.tensor_copy(fetched[1], yn[t][:].indirect(entries("n3", lo, hi)))
+            nc.vector.tensor_tensor(left, y[t][:].indirect(entries("n2", lo, hi)), fetched[0], MULT)
+            nc.vector.tensor_tensor(right, y[t][:].indirect(entries("n4", lo, hi)), fetched[1], MULT)
 
         z_words = tile([P, S], U32, "z_words")
         z_scales = tile([P, S], U8, "z_scales")
         s = [tile([P, S], F32, "s%d" % t) for t in range(PACK)]
         sq = [tile([P, S], F32, "sq%d" % t) for t in range(PACK)]
         s_banks = [psum.tile([P, S], F32, name="s_bank%d" % t) for t in range(PACK)]
-        for lo, hi in PIECES:
-            width = hi - lo
-            z = tile([P, PACK * width], F32, "z%d" % lo)
-            pending = []
-            joiner = nc.vector if hi == S else nc.gpsimd
-            for t in range(PACK):
-                f1, p12, p34 = [tile([P, width], F32, "%s_%d_%d" % (n, lo, t)) for n in ("f1", "p12", "p34")]
-                f3 = tile([P, width], F32, "f3_%d_%d" % (lo, t), "z_grouped0" if lo > 0 and t == 3 else None)
-                nc.vector.tensor_copy(f1[:], yg[t][:].indirect(entries("n1", lo, hi)))
-                for args in pending:
-                    joiner.tensor_tensor(*args)
-                nc.vector.tensor_copy(f3[:], yg[t][:].indirect(entries("n3", lo, hi)))
-                nc.vector.tensor_tensor(p12[:], y[t][:].indirect(entries("n2", lo, hi)), f1[:], MULT)
-                nc.vector.tensor_tensor(p34[:], y[t][:].indirect(entries("n4", lo, hi)), f3[:], MULT)
-                pending = [(z[:, t * width : (t + 1) * width], p12[:], p34[:], SUB)]
-            joiner.tensor_tensor(*pending[0])
-            grouped = interleave(z, width, hi == S, "z_grouped%d" % lo)
-            quantize(z_words, z_scales, grouped, lo, width)
-            for t in range(PACK):
-                for a, b in SPANS[width]:
-                    nc.tensor.matmul_mx(
-                        out=s_banks[t][:, lo + a : lo + b],
-                        lhsT=cand_words[:, P * t : P * (t + 1)].bitcast(FP8X4),
-                        lhsT_scale=cand_scales[:, P * t : P * (t + 1)],
-                        rhs=z_words[:, lo + a : lo + b].bitcast(FP8X4),
-                        rhs_scale=z_scales[:, lo + a : lo + b],
-                        start=True,
-                        stop=True,
-                    )
-                if t == 0:
-                    nc.scalar.activation(sq[t][:, lo:hi], s_banks[t][:, lo:hi], COPY, scale=0.75 * 0.0625)
-                    nc.scalar.activation(s[t][:, lo:hi], s_banks[t][:, lo:hi], COPY, scale=0.0625)
-        for t in range(1, PACK):
-            nc.scalar.activation(sq[t][:], s_banks[t][:], COPY, scale=0.75 * 0.0625)
-            nc.scalar.activation(s[t][:], s_banks[t][:], COPY, scale=0.0625)
+
+        def score(t, lo, hi):
+            nc.tensor.matmul_mx(
+                out=s_banks[t][:, lo:hi],
+                lhsT=cand_words[:, P * t : P * (t + 1)].bitcast(FP8X4),
+                lhsT_scale=cand_scales[:, P * t : P * (t + 1)],
+                rhs=z_words[:, lo:hi].bitcast(FP8X4),
+                rhs_scale=z_scales[:, lo:hi],
+                start=True,
+                stop=True,
+            )
+            nc.scalar.activation(sq[t][:, lo:hi], s_banks[t][:, lo:hi], COPY, scale=0.75 * 0.0625)
+            nc.scalar.activation(s[t][:, lo:hi], s_banks[t][:, lo:hi], COPY, scale=0.0625)
+
+        def z_quantized(lo, hi, total):
+            if hi == HALF:
+                score(0, 0, HALF)
+            if hi == S:
+                score(0, HALF, S)
+                for t in range(1, PACK):
+                    score(t, 0, S)
+
+        join(z_products, 2, "z", z_words, z_scales, lambda sums, t: None, z_quantized)
+
+        def out_products(t, lo, hi, left, right, fetched):
+            nc.vector.tensor_copy(fetched[0], sq[t][:].indirect(entries("n6", lo, hi)))
+            nc.vector.tensor_tensor(left, s[t][:].indirect(entries("n5", lo, hi)), sq[t][:, lo:hi], MULT)
+            nc.vector.tensor_tensor(right, s[t][:].indirect(entries("n7", lo, hi)), fetched[0], MULT)
 
         o_words = tile([P, S], U32, "o_words")
         o_scales = tile([P, S], U8, "o_scales")
         out_rows = out_0.rearrange("(p t) j -> p t j", t=PACK)
         out_words = out_1[0].rearrange("p n t -> p (n t)").bitcast(I32)
-        for lo, hi in PIECES:
-            width = hi - lo
-            o = tile([P, PACK * width], F32, "o%d" % lo)
-            pending = []
-            joiner = nc.vector if hi == S else nc.gpsimd
-            for t in range(PACK):
-                f6, p5 = [tile([P, width], F32, "%s_%d_%d" % (n, lo, t)) for n in ("f6", "p5")]
-                p67 = tile([P, width], F32, "p67_%d_%d" % (lo, t), "o_grouped0" if lo > 0 and t == 3 else None)
-                nc.vector.tensor_copy(f6[:], sq[t][:].indirect(entries("n6", lo, hi)))
-                for args in pending:
-                    joiner.tensor_tensor(*args)
-                nc.vector.tensor_tensor(p5[:], s[t][:].indirect(entries("n5", lo, hi)), sq[t][:, lo:hi], MULT)
-                nc.vector.tensor_tensor(p67[:], s[t][:].indirect(entries("n7", lo, hi)), f6[:], MULT)
-                pending = [(o[:, t * width : (t + 1) * width], p5[:], p67[:], ADD)]
-            joiner.tensor_tensor(*pending[0])
-            nc.sync.dma_start(out_rows[:, :, lo:hi], o[:].rearrange("p (t j) -> p t j", t=PACK))
-            grouped = interleave(o, width, hi == S, "o_grouped%d" % lo)
-            quantize(o_words, o_scales, grouped, lo, width)
-            nc.sync.dma_start(out_words[:, lo:hi], o_words[:].bitcast(I32)[:, lo:hi])
+
+        def store_rows(sums, t):
+            rows = tile([P, WIDE], F32, "o_rows%d" % t)
+            for c in range(CHUNKS):
+                nc.scalar.copy(rows[:, c * P : (c + 1) * P], sums[c][:, t * P : (t + 1) * P])
+            nc.sync.dma_start(out_rows[:, t, 0:WIDE], rows[:])
+
+        def out_quantized(lo, hi, total):
+            if hi == HALF:
+                nc.sync.dma_start(out_words[:, 0:HALF], o_words[:].bitcast(I32)[:, 0:HALF])
+            if hi == S:
+                by_tile = total[:].rearrange("p (t j) -> p t j", t=PACK)
+                nc.sync.dma_start(out_rows[:, 0 : PACK - 1, WIDE:S], by_tile[:, 0 : PACK - 1, :])
+                nc.sync.dma_start(out_rows[:, PACK - 1, WIDE:S], by_tile[:, PACK - 1, :])
+                nc.sync.dma_start(out_words[:, HALF:S], o_words[:].bitcast(I32)[:, HALF:S])
+
+        join(out_products, 1, "o", o_words, o_scales, store_rows, out_quantized)
         out_scale_rows = out_2[0].bitcast(I32)
         for q in range(4):
-            queue = nc.scalar if q % 2 == 0 else nc.sync
+            queue = nc.sync if q == 3 else nc.scalar
             queue.dma_start(out_scale_rows[4 * q : 4 * q + 4, :], o_scales[:].bitcast(I32)[32 * q : 32 * q + 4, :])

from contextlib import ExitStack

import concourse.mybir as mybir
from concourse.masks import make_identity

F32 = mybir.dt.float32
BF16 = mybir.dt.bfloat16
I32 = mybir.dt.int32
U32 = mybir.dt.uint32
U16 = mybir.dt.uint16
U8 = mybir.dt.uint8
FP8X4 = mybir.dt.float8_e4m3fn_x4
FP4X4 = mybir.dt.float4_e2m1fn_x4
MULT = mybir.AluOpType.mult
ADD = mybir.AluOpType.add
COPY = mybir.ActivationFunctionType.Copy

P = 128
PACK = 4
T = 2048
S = 512
FLOPS = 2 * 2 * 512 * 512 * 512

CHUNKS = 3
WIDE = CHUNKS * P
HALF = 256


def tile_picked_hcanddetdot_none_po_kernel(
    tc, x_words, x_scales, w1_words, w1_scales, gs, offs, n1, n2, n3, n4, cand, n5, n6, n7, out_0, out_1, out_2
):
    nc = tc.nc
    with ExitStack() as ctx:
        keep = ctx.enter_context(tc.tile_pool(name="keep", bufs=1))
        psum = ctx.enter_context(tc.psum_pool(name="psum", bufs=1))

        def tile(shape, dtype, name, tag=None):
            return keep.tile(shape, dtype, name=name, tag=tag or name, align_bytes=64)

        lists = {}

        def load_list(name, source):
            lists[name] = tile([P, S // 16], U16, "list_" + name)
            nc.sync.dma_start(lists[name][:], source)

        def entries(name, lo, hi):
            return lists[name][:, lo // 16 : hi // 16]

        table_scales = tile([P, T], U8, "table_scales")
        table_words = tile([P, T], U32, "table_words")
        w_words_in = tile([P, 2 * S], U8, "w_words_in")
        w_scales_in = tile([P, S], U8, "w_scales_in")
        place_scales = tile([P, S], U8, "place_scales")
        cand_scales = tile([P, S], U8, "cand_scales")
        gain_in = tile([P, PACK], F32, "gain_in")
        gain = tile([P, PACK], F32, "gain")
        minus_gain = tile([P, PACK], F32, "minus_gain")

        for plane in (table_scales, w_scales_in, place_scales, cand_scales):
            nc.gpsimd.memset(plane[:].bitcast(I32), 0)

        nc.sync.dma_start(w_words_in[:].bitcast(I32), w1_words[0].bitcast(I32))
        load_list("offs", offs)
        nc.sync.dma_start(table_scales[:].bitcast(I32)[0:P:8, :], x_scales[0].bitcast(I32))
        load_list("cand", cand)
        nc.sync.dma_start(gain_in[:], gs.rearrange("(p t) o -> p (t o)", t=PACK))
        load_list("n1", n1)
        load_list("n3", n3)
        nc.sync.dma_start(table_words[:].bitcast(I32), x_words[0].rearrange("p n t -> p (n t)").bitcast(I32))
        w_rows = w1_scales[0].bitcast(I32)
        for a in range(4):
            nc.sync.dma_start(w_scales_in[:].bitcast(I32)[a:P:32, :], w_rows[a:16:4, :])
        nc.scalar.activation(gain[:], gain_in[:], COPY, scale=0.75)
        nc.scalar.activation(minus_gain[:], gain_in[:], COPY, scale=-0.75)
        identity = tile([P, P], F32, "identity")
        make_identity(nc, identity[:])

        w_words = tile([P, 2 * S], U8, "w_words")
        w_scales = tile([P, S], U8, "w_scales")
        nc.vector.tensor_copy(
            w_words[:].rearrange("p (t m b) -> p t m b", t=PACK, b=2),
            w_words_in[:].rearrange("p (m t b) -> p t m b", t=PACK, b=2),
        )

        def place_rows(plane, gathered, queues):
            for a in range(4):
                queues[a % len(queues)].dma_start(plane[:].bitcast(I32)[a:P:32, :], gathered[:].bitcast(I32)[8 * a : P : 32, :])

        place_bytes = tile([P, S], U8, "place_bytes")
        nc.vector.tensor_copy(place_bytes[:], table_scales[:].indirect(lists["offs"][:]))
        place_rows(place_scales, place_bytes, (nc.scalar,))

        for name, source in (("n2", n2), ("n4", n4)):
            load_list(name, source)

        place_words = tile([P, S], U32, "place_words")
        nc.vector.tensor_copy(place_words[:], table_words[:].indirect(lists["offs"][:]))
        nc.vector.tensor_copy(
            w_scales[:].rearrange("p (t m) -> p t m", t=PACK), w_scales_in[:].rearrange("p (m t) -> p t m", t=PACK)
        )

        y = [tile([P, S], F32, "y%d" % t) for t in range(PACK)]
        yg = [tile([P, S], F32, "yg%d" % t) for t in range(PACK)]
        yn = [tile([P, S], F32, "yn%d" % t) for t in range(PACK)]
        for t in range(PACK):
            bank = psum.tile([P, S], F32, name="y_bank%d" % t, tag="bank%d" % t)
            nc.tensor.matmul_mx(
                out=bank[:],
                lhsT=w_words[:, 2 * P * t : 2 * P * (t + 1)].bitcast(FP4X4),
                lhsT_scale=w_scales[:, P * t : P * (t + 1)],
                rhs=place_words[:].bitcast(FP8X4),
                rhs_scale=place_scales[:],
                start=True,
                stop=True,
            )
            nc.scalar.activation(yg[t][:], bank[:], COPY, scale=gain[:, t : t + 1])
            nc.scalar.activation(yn[t][:], bank[:], COPY, scale=minus_gain[:, t : t + 1])
            nc.scalar.copy(y[t][:], bank[:])

        cand_bytes = tile([P, S], U8, "cand_bytes")
        cand_bytes_dealt = tile([P, S], U8, "cand_bytes_dealt")
        cand_picked = tile([P, S], U32, "cand_picked", "w_scales_in")
        cand_words = tile([P, S], U32, "cand_words")
        nc.vector.tensor_copy(cand_bytes[:], table_scales[:].indirect(lists["cand"][:]))
        nc.vector.tensor_copy(cand_picked[:], table_words[:].indirect(lists["cand"][:]))
        nc.vector.tensor_copy(
            cand_bytes_dealt[:].rearrange("p (t m) -> p t m", t=PACK), cand_bytes[:].rearrange("p (m t) -> p t m", t=PACK)
        )
        nc.vector.tensor_copy(
            cand_words[:].rearrange("p (t m) -> p t m", t=PACK), cand_picked[:].rearrange("p (m t) -> p t m", t=PACK)
        )
        place_rows(cand_scales, cand_bytes_dealt, (nc.sync,))
        for name, source in (("n6", n6), ("n5", n5), ("n7", n7)):
            load_list(name, source)

        def quantize(words, scales, grouped, lo, hi):
            nc.vector.quantize_mx(out=words[:, lo:hi].bitcast(FP8X4), scales=scales[:, lo:hi], in_=grouped[:])

        def add_on_tensor(left, right, t, sums, name):
            turned = psum.tile([P, WIDE], F32, name=name + "_turned%d" % t, tag="bank0")
            for c in range(CHUNKS):
                cols = slice(c * P, (c + 1) * P)
                nc.tensor.matmul(turned[:, cols], left[:, cols], identity[:], start=True, stop=False, is_transpose=True)
                nc.tensor.matmul(turned[:, cols], right[:, cols], identity[:], start=False, stop=True, is_transpose=True)
            staged = tile([P, WIDE], F32, name + "_staged%d" % t)
            nc.scalar.copy(staged[:], turned[:])
            for c in range(CHUNKS):
                nc.tensor.transpose(sums[c][:, t * P : (t + 1) * P], staged[:, c * P : (c + 1) * P], identity[:])

        def join(products, copies, name, words, scales, store_rows, quantized):
            sums = [psum.tile([P, PACK * P], F32, name=name + "_sums%d" % c, tag="bank%d" % (c + 1)) for c in range(CHUNKS)]
            for t in range(PACK):
                left = tile([P, WIDE], F32, name + "_left%d" % t)
                right = tile([P, WIDE], F32, name + "_right%d" % t)
                fetched = [tile([P, WIDE], F32, name + "_fetched%d_%d" % (t, k)) for k in range(copies)]
                products(t, 0, WIDE, left[:], right[:], [f[:] for f in fetched])
                add_on_tensor(left, right, t, sums, name)
                if t < PACK - 1:
                    store_rows(sums, t)
            for lo, hi in ((0, HALF), (HALF, WIDE)):
                grouped = tile([P, (hi - lo) * PACK], BF16, name + "_grouped%d" % lo)
                for c in range(lo // P, hi // P):
                    nc.scalar.copy(
                        grouped[:, (c * P - lo) * PACK : ((c + 1) * P - lo) * PACK].rearrange("p (j t) -> p j t", t=PACK),
                        sums[c][:].rearrange("p (t j) -> p j t", t=PACK),
                    )
                quantize(words, scales, grouped, lo, hi)
                quantized(lo, hi, None)
            store_rows(sums, PACK - 1)

            work = tile([P, (2 + copies) * S], F32, name + "_last_work", name + "_fetched%d_0" % (PACK - 1))
            left, right = work[:, 0:S], work[:, S : 2 * S]
            final_right = tile([P, P], F32, name + "_final_right", name + "_grouped0")
            total = tile([P, PACK * P], F32, name + "_last_total")
            early = slice(0, (PACK - 1) * P)
            for t in range(PACK):
                cols = slice(t * P, (t + 1) * P)
                fetched = [work[:, (2 + k) * S + t * P : (2 + k) * S + (t + 1) * P] for k in range(copies)]
                products(t, WIDE, S, left[:, cols], right[:, cols] if t < PACK - 1 else final_right[:], fetched)
                if t == PACK - 2:
                    nc.vector.tensor_tensor(total[:, early], left[:, early], right[:, early], ADD)
            nc.vector.tensor_tensor(total[:, cols], left[:, cols], final_right[:], ADD)
            grouped = tile([P, P * PACK], BF16, name + "_last_grouped", name + "_grouped%d" % HALF)
            nc.vector.tensor_copy(
                grouped[:].rearrange("p (c i t) -> p c t i", i=4, t=PACK),
                total[:].rearrange("p (t c i) -> p c t i", i=4, t=PACK),
            )
            quantize(words, scales, grouped, WIDE, S)
            quantized(WIDE, S, total)

        def z_products(t, lo, hi, left, right, fetched):
            nc.vector.tensor_copy(fetched[0], yg[t][:].indirect(entries("n1", lo, hi)))
            nc.vector.tensor_copy(fetched[1], yn[t][:].indirect(entries("n3", lo, hi)))
            nc.vector.tensor_tensor(left, y[t][:].indirect(entries("n2", lo, hi)), fetched[0], MULT)
            nc.vector.tensor_tensor(right, y[t][:].indirect(entries("n4", lo, hi)), fetched[1], MULT)

        z_words = tile([P, S], U32, "z_words")
        z_scales = tile([P, S], U8, "z_scales")
        s = [tile([P, S], F32, "s%d" % t) for t in range(PACK)]
        sq = [tile([P, S], F32, "sq%d" % t) for t in range(PACK)]
        s_banks = [psum.tile([P, S], F32, name="s_bank%d" % t) for t in range(PACK)]

        def score(t, lo, hi):
            nc.tensor.matmul_mx(
                out=s_banks[t][:, lo:hi],
                lhsT=cand_words[:, P * t : P * (t + 1)].bitcast(FP8X4),
                lhsT_scale=cand_scales[:, P * t : P * (t + 1)],
                rhs=z_words[:, lo:hi].bitcast(FP8X4),
                rhs_scale=z_scales[:, lo:hi],
                start=True,
                stop=True,
            )
            nc.scalar.activation(sq[t][:, lo:hi], s_banks[t][:, lo:hi], COPY, scale=0.75 * 0.0625)
            nc.scalar.activation(s[t][:, lo:hi], s_banks[t][:, lo:hi], COPY, scale=0.0625)

        def z_quantized(lo, hi, total):
            if hi == HALF:
                score(0, 0, HALF)
            if hi == S:
                score(0, HALF, S)
                for t in range(1, PACK):
                    score(t, 0, S)

        join(z_products, 2, "z", z_words, z_scales, lambda sums, t: None, z_quantized)

        def out_products(t, lo, hi, left, right, fetched):
            nc.vector.tensor_copy(fetched[0], sq[t][:].indirect(entries("n6", lo, hi)))
            nc.vector.tensor_tensor(left, s[t][:].indirect(entries("n5", lo, hi)), sq[t][:, lo:hi], MULT)
            nc.vector.tensor_tensor(right, s[t][:].indirect(entries("n7", lo, hi)), fetched[0], MULT)

        o_words = tile([P, S], U32, "o_words")
        o_scales = tile([P, S], U8, "o_scales")
        out_rows = out_0.rearrange("(p t) j -> p t j", t=PACK)
        out_words = out_1[0].rearrange("p n t -> p (n t)").bitcast(I32)

        def store_rows(sums, t):
            rows = tile([P, WIDE], F32, "o_rows%d" % t)
            for c in range(CHUNKS):
                nc.scalar.copy(rows[:, c * P : (c + 1) * P], sums[c][:, t * P : (t + 1) * P])
            nc.sync.dma_start(out_rows[:, t, 0:WIDE], rows[:])

        def out_quantized(lo, hi, total):
            if hi == HALF:
                nc.sync.dma_start(out_words[:, 0:HALF], o_words[:].bitcast(I32)[:, 0:HALF])
            if hi == S:
                by_tile = total[:].rearrange("p (t j) -> p t j", t=PACK)
                nc.sync.dma_start(out_rows[:, 0 : PACK - 1, WIDE:S], by_tile[:, 0 : PACK - 1, :])
                nc.sync.dma_start(out_rows[:, PACK - 1, WIDE:S], by_tile[:, PACK - 1, :])
                nc.sync.dma_start(out_words[:, HALF:S], o_words[:].bitcast(I32)[:, HALF:S])

        join(out_products, 1, "o", o_words, o_scales, store_rows, out_quantized)
        out_scale_rows = out_2[0].bitcast(I32)
        for q in range(4):
            queue = nc.sync if q == 3 else nc.scalar
            queue.dma_start(out_scale_rows[4 * q : 4 * q + 4, :], o_scales[:].bitcast(I32)[32 * q : 32 * q + 4, :])
